import numpy as np
import ml_dtypes


def mxq(x, axis, fmt="e4m3"):
    dtype, down = {"e4m3": (ml_dtypes.float8_e4m3fn, 7), "e5m2": (ml_dtypes.float8_e5m2, 14)}[fmt]
    v = np.moveaxis(np.asarray(x, np.float32).astype(ml_dtypes.bfloat16).astype(np.float64), axis, -1)
    blocks = v.reshape(v.shape[:-1] + (-1, 32))
    amax = np.abs(blocks).max(-1, keepdims=True)
    byte = np.maximum(np.where(amax > 0, np.frexp(amax)[1] - 1 + 127, 0) - down, 1)
    scale = np.exp2(byte - 127.0)
    codes = (blocks / scale).astype(np.float32).astype(dtype).astype(np.float64)
    return np.moveaxis((codes * scale).reshape(v.shape), -1, axis)


WIDE = False


def mx_kscale(k):
    if not WIDE:
        return np.ones(k)
    levels = np.array([10, -10, 5, -5, 0])
    if k % 512:
        return np.exp2(np.random.permutation(np.resize(levels, k // 32))).repeat(32)
    a = np.empty((k // 512, 16))
    for p in range(k // 512):
        a[p, :8] = np.random.permutation(np.resize(levels, 8))
        for g in range(8):
            far = levels[np.abs(levels - a[p, g]) >= 10]
            a[p, g + 8] = far[np.random.randint(len(far))]
    return np.exp2(a.ravel()).repeat(32)


def f64(x):
    return np.asarray(x).astype(np.float64)


def striped(idx):
    return np.tile(idx.reshape(-1, 16).T, (8, 1)).astype(np.uint16)


def unstriped(offs):
    return offs[:16].T.reshape(-1).astype(np.int64)


E2M1 = np.array([0.0, 0.5, 1.0, 1.5, 2.0, 3.0, 4.0, 6.0, -0.0, -0.5, -1.0, -1.5, -2.0, -3.0, -4.0, -6.0])


def pack_weight(w, fmt):
    k, n = w.shape
    w = f64(np.asarray(w, np.float32).astype(ml_dtypes.bfloat16)).reshape(k // 32, 32, n)
    amax = np.abs(w).max(1)
    if fmt == "e4m3":
        byte = np.frexp(amax)[1] - 1 + 127 - 7
    else:
        mant, ex = np.frexp(amax / 6.0)
        byte = np.where(mant > 0.5, ex, ex - 1) + 127
    byte = np.clip(np.where(amax > 0, byte, 1), 1, 254)
    scaled = (w * np.exp2(127.0 - byte)[:, None, :]).reshape(k, n).astype(np.float32)
    by_word = np.ascontiguousarray(scaled.reshape(k // 512, 128, 4, n).transpose(0, 1, 3, 2))
    if fmt == "e4m3":
        words = by_word.astype(ml_dtypes.float8_e4m3fn).view(np.uint8)
    else:
        c = by_word.astype(ml_dtypes.float4_e2m1fn).view(np.uint8) & 0xF
        words = (c[..., 0::2] | (c[..., 1::2] << 4)).reshape(k // 512, 128, 2 * n)
    return np.ascontiguousarray(words), np.ascontiguousarray(byte.astype(np.uint8).reshape(k // 512, 16, n))


def unpack_weight(words, scales, fmt):
    g, _, n = scales.shape
    words = np.ascontiguousarray(words).reshape(g, 128, n, -1)
    if fmt == "e4m3":
        vals = words.view(ml_dtypes.float8_e4m3fn).astype(np.float64)
    else:
        nib = np.empty((g, 128, n, 4), np.uint8)
        nib[..., 0::2] = words & 0xF
        nib[..., 1::2] = words >> 4
        vals = E2M1[nib]
    vals = vals * np.repeat(np.exp2(scales.astype(np.float64) - 127.0), 8, axis=1)[..., None]
    return vals.transpose(0, 1, 3, 2).reshape(g * 512, n)


def gelu(v):
    return 0.5 * v * (1.0 + np.tanh(np.sqrt(2.0 / np.pi) * (v + 0.044715 * v**3)))


K, T, S, H, P, N = 1024, 4096, 1024, 512, 512, 768

def setup_inputs():
    n = np.random.standard_normal
    s = mx_kscale(K)[:, None]
    u = mx_kscale(H)[:, None]
    tab_words, tab_scales = pack_weight(n((K, T)) * s, "e4m3")
    w3_words, w3_scales = pack_weight(0.7 * n((K, H)) / s / np.sqrt(K), "e2m1")
    wb_words, wb_scales = pack_weight(n((H, N)) / u / np.sqrt(H), "e4m3")
    return {
        "tab_words": tab_words, "tab_scales": tab_scales,
        "offs": striped(np.random.permutation(T)[:S]),
        "pos1": striped(np.random.permutation(S)[:P]),
        "pos2": striped(np.random.permutation(S)[:P]),
        "w1": (n((K, H)) / s / np.sqrt(K)).astype(np.float32),
        "w2": (0.55 * n((K, H)) / s / np.sqrt(K)).astype(np.float32),
        "w3_words": w3_words, "w3_scales": w3_scales,
        "gain": (np.exp(0.3 * n(H)) * u[:, 0]).astype(np.float32),
        "base": (0.8 * n((H, P)) * u).astype(np.float32),
        "wa": (n((H, N)) / u / np.sqrt(H)).astype(np.float32),
        "wb_words": wb_words, "wb_scales": wb_scales,
        "bo": (0.5 * n(N)).astype(np.float32),
    }

def reference(tab_words, tab_scales, offs, pos1, pos2, w1, w2, w3_words, w3_scales,
              gain, base, wa, wb_words, wb_scales, bo):
    v = unpack_weight(tab_words, tab_scales, "e4m3")[:, unstriped(offs)]
    w3 = unpack_weight(w3_words, w3_scales, "e2m1")
    wb = unpack_weight(wb_words, wb_scales, "e4m3")
    size = mxq(f64(w1), 0, "e4m3").T @ v
    phase = mxq(f64(w2), 0, "e4m3").T @ v
    level = w3.T @ v
    h = (size * np.cos(phase) + level) * f64(gain)[:, None]
    xa = mxq(np.abs(h[:, unstriped(pos1)]), 0, "e4m3")
    xb = mxq(h[:, unstriped(pos2)] + f64(base), 0, "e4m3")
    y = mxq(f64(wa), 0, "e4m3").T @ xa + wb.T @ xb
    return y + f64(bo)[:, None]

@@ -1,0 +1,277 @@
+import math
+from contextlib import ExitStack
+
+import concourse.mybir as mybir
+
+K, T, S, H, M, N = 1024, 4096, 1024, 512, 512, 768
+FLOPS = 2 * (3 * K * H * S + 2 * H * N * M)
+
+F32 = mybir.dt.float32
+BF16 = mybir.dt.bfloat16
+I32 = mybir.dt.int32
+U32 = mybir.dt.uint32
+U16 = mybir.dt.uint16
+U8 = mybir.dt.uint8
+FP8X4 = mybir.dt.float8_e4m3fn_x4
+FP4X4 = mybir.dt.float4_e2m1fn_x4
+ALU = mybir.AluOpType
+ACT = mybir.ActivationFunctionType
+
+P = 128
+PACK = 4
+K_PASS = P * PACK
+PASSES = K // K_PASS
+BANK = 512
+HALVES = S // BANK
+CHUNK = 256
+CHUNKS = M // CHUNK
+N_TILES = N // P
+
+
+def tile_list_doppler_beat_features_kernel(
+    tc, tab_words, tab_scales, offs, pos1, pos2, w1, w2, w3_words, w3_scales, gain, base, wa, wb_words, wb_scales, bo, out
+):
+    nc = tc.nc
+    with ExitStack() as ctx:
+        keep = ctx.enter_context(tc.tile_pool(name="keep", bufs=1))
+        psum = ctx.enter_context(tc.psum_pool(name="psum", bufs=1))
+
+        def sb(name, shape, dtype):
+            return keep.tile(shape, dtype, name=name, align_bytes=64)
+
+        idx = keep.tile([P, S // 16], U16, name="idx")
+        p1 = keep.tile([P, M // 16], U16, name="p1")
+        p2 = keep.tile([P, M // 16], U16, name="p2")
+
+        tab_sc = sb("tab_sc", [P, T], U8)
+        v_sc = sb("v_sc", [P, S], U8)
+        v_sc1 = sb("v_sc1", [P, S], U8)
+        w3_sc_raw = sb("w3_sc_raw", [P, PASSES * H], U8)
+        wb_sc = sb("wb_sc", [P, N], U8)
+        for plane in (tab_sc, w3_sc_raw, v_sc1, wb_sc):
+            nc.vector.memset(plane[:].bitcast(I32), 0)
+
+        def load_rows(name, rows):
+            raw = sb(name, [P, PACK, rows.shape[1]], F32)
+            nc.sync.dma_start(out=raw[:], in_=rows.rearrange("(p j) w -> p j w", j=PACK))
+            return raw
+
+        def load_words(name, words):
+            flat = words.rearrange("p t i -> p (t i)").bitcast(I32)
+            tile = sb(name, [P, flat.shape[1]], I32)
+            nc.sync.dma_start(out=tile[:], in_=flat)
+            return tile
+
+        w2_raw = [load_rows("w2_raw%d" % a, w2[a * K_PASS : (a + 1) * K_PASS, :]) for a in range(PASSES)]
+        nc.sync.dma_start(idx[:], offs)
+        w3_raw = sb("w3_raw", [P, PASSES, 2 * H], U8)
+        nc.sync.dma_start(out=w3_raw[:].bitcast(I32), in_=w3_words.bitcast(I32).rearrange("a p c -> p a c"))
+        gain_sb = sb("gain_sb", [P, PACK], F32)
+        nc.sync.dma_start(out=gain_sb[:], in_=gain.rearrange("(p t) -> p t", t=PACK))
+        nc.sync.dma_start(p1[:], pos1)
+        nc.sync.dma_start(p2[:], pos2)
+        tab = [load_words("tab%d" % a, tab_words[a]) for a in range(PASSES)]
+        w1_raw0 = load_rows("w1_raw0", w1[0:K_PASS, :])
+        w1_raw1 = [load_rows("w1_raw1_%d" % u, w1[K_PASS:K, u * (H // 2) : (u + 1) * (H // 2)]) for u in range(2)]
+        wa_raw = load_rows("wa_raw", wa)
+        base_sb = load_rows("base_sb", base)
+        wb_codes = load_words("wb_codes", wb_words[0])
+        for q in range(4):
+            nc.sync.dma_start(
+                out=wb_sc[32 * q : 32 * q + 4, :].bitcast(I32), in_=wb_scales[0, 4 * q : 4 * q + 4, :].bitcast(I32)
+            )
+        bo_sb = sb("bo_sb", [P, N_TILES], F32)
+        with nc.allow_non_contiguous_dma(reason="one bias value a partition and output tile"):
+            nc.sync.dma_start(out=bo_sb[:], in_=bo.rearrange("(c p) -> p c", p=P))
+
+        for q in range(4):
+            nc.gpsimd.dma_start(
+                out=tab_sc[32 * q : 32 * q + 4 * PASSES, :].bitcast(I32),
+                in_=tab_scales[:, 4 * q : 4 * q + 4, :].bitcast(I32),
+            )
+        for q in range(4):
+            nc.gpsimd.dma_start(
+                out=w3_sc_raw[32 * q : 32 * q + 4, :].bitcast(I32).rearrange("r (a c) -> r a c", a=PASSES),
+                in_=w3_scales[:, 4 * q : 4 * q + 4, :].bitcast(I32).rearrange("a r c -> r a c"),
+            )
+
+        def deal(engine_copy, grouped, raw, m0):
+            ms = raw.shape[2] // PACK
+            engine_copy(
+                out=grouped[:].rearrange("p (t m j) -> p m t j", t=PACK, j=PACK)[:, m0 : m0 + ms, :, :],
+                in_=raw[:].rearrange("p j (m t) -> p m t j", t=PACK),
+            )
+
+        def quantize(codes, scales, grouped):
+            nc.vector.quantize_mx(out=codes.bitcast(FP8X4), scales=scales, in_=grouped)
+
+        w_codes, w_sc, w_bf = {}, {}, {}
+        for name in ("w1", "w2"):
+            for a in range(PASSES):
+                w_codes[name, a] = sb("%s_codes%d" % (name, a), [P, H], U32)
+                w_sc[name, a] = sb("%s_sc%d" % (name, a), [P, H], U8)
+                w_bf[name, a] = sb("%s_bf%d" % (name, a), [P, PACK * H], BF16)
+
+        w3_codes = sb("w3_codes", [P, PASSES, PACK, 2 * P], U8)
+        w3_sc = sb("w3_sc", [P, PASSES, PACK, P], U8)
+        for a in range(PASSES):
+            deal(nc.scalar.copy, w_bf["w2", a], w2_raw[a], 0)
+        nc.vector.tensor_copy(
+            out=w3_codes[:].rearrange("p a t (m b) -> p a t m b", b=2),
+            in_=w3_raw[:].rearrange("p a (m t b) -> p a t m b", t=PACK, b=2),
+        )
+        nc.gpsimd.tensor_copy(out=w3_sc[:], in_=w3_sc_raw[:].rearrange("p (a m t) -> p a t m", a=PASSES, t=PACK))
+        nc.vector.tensor_copy(out=v_sc[:], in_=tab_sc[:].indirect(idx[:]))
+        for q in range(4):
+            nc.gpsimd.dma_start(
+                out=v_sc1[32 * q : 32 * q + 4, :].bitcast(I32), in_=v_sc[32 * q + 4 : 32 * q + 8, :].bitcast(I32)
+            )
+        for a in range(PASSES):
+            quantize(w_codes["w2", a][:], w_sc["w2", a][:], w_bf["w2", a][:])
+
+        v_codes = {}
+        for a in range(PASSES):
+            for u in range(HALVES):
+                v_codes[a, u] = sb("v_codes%d_%d" % (a, u), [P, BANK], U32)
+                cols = slice(u * BANK // 16, (u + 1) * BANK // 16)
+                nc.vector.tensor_copy(out=v_codes[a, u][:], in_=tab[a][:].bitcast(U32).indirect(idx[:, cols]))
+
+        def first_stage(name, t, u, bufs):
+            acc = psum.tile([P, BANK], F32, name="acc_" + name, tag=name, bufs=bufs)
+            cols = slice(u * BANK, (u + 1) * BANK)
+            for a in range(PASSES):
+                if name == "w3":
+                    lhsT = w3_codes[:, a, t, :].bitcast(FP4X4)
+                    lhsT_scale = w3_sc[:, a, t, :]
+                    rhs_scale = (v_sc, v_sc1)[a][:, cols]
+                else:
+                    lhsT = w_codes[name, a][:, t * P : (t + 1) * P].bitcast(FP8X4)
+                    lhsT_scale = w_sc[name, a][:, t * P : (t + 1) * P]
+                    rhs_scale = v_sc[4 * a : P, cols]
+                nc.tensor.matmul_mx(
+                    out=acc[:], lhsT=lhsT, lhsT_scale=lhsT_scale, rhs=v_codes[a, u][:].bitcast(FP8X4),
+                    rhs_scale=rhs_scale, start=(a == 0), stop=(a == PASSES - 1),
+                )
+            return acc
+
+        cos = [sb("cos%d" % t, [P, S], F32) for t in range(PACK)]
+        for t in range(PACK):
+            folded = keep.tile([P, S], F32, name="folded", tag="scalar_stage%d" % (t % 2), align_bytes=64)
+            for u in range(HALVES):
+                phase = first_stage("w2", t, u, 2)
+                nc.scalar.activation(out=folded[:, u * BANK : (u + 1) * BANK], in_=phase[:], func=ACT.Abs)
+            nc.scalar.activation(out=cos[t][:], in_=folded[:], func=ACT.Sin, bias=math.pi / 2, scale=-1.0)
+
+        deal(nc.vector.tensor_copy, w_bf["w1", 0], w1_raw0, 0)
+        quantize(w_codes["w1", 0][:], w_sc["w1", 0][:], w_bf["w1", 0][:])
+        for u in range(2):
+            deal(nc.vector.tensor_copy, w_bf["w1", 1], w1_raw1[u], u * (P // 2))
+        for t in range(PACK):
+            quantize(
+                w_codes["w1", 1][:, t * P : (t + 1) * P], w_sc["w1", 1][:, t * P : (t + 1) * P],
+                w_bf["w1", 1][:, t * K_PASS : (t + 1) * K_PASS],
+            )
+
+        def weave_views(grouped, planes):
+            return (
+                grouped.rearrange("p (c i t) -> p c t i", i=4, t=PACK),
+                planes.rearrange("p t (c i) -> p c t i", i=4),
+            )
+
+        wa_bf = keep.tile([P, PACK * N], BF16, name="wa_bf", tag="scalar_stage1", align_bytes=64)
+        wa_codes = sb("wa_codes", [P, N], U32)
+        wa_sc = sb("wa_sc", [P, N], U8)
+        dst, src = weave_views(wa_bf[:], wa_raw[:])
+        nc.scalar.copy(out=dst, in_=src)
+
+        h = [sb("h%d" % t, [P, S], F32) for t in range(PACK)]
+        xa = sb("xa", [P, PACK, M], F32)
+        xb = [sb("xb%d" % c, [P, PACK, CHUNK], F32) for c in range(CHUNKS)]
+
+        def pick_a(t):
+            nc.vector.tensor_copy(out=xa[:, t, :], in_=h[t][:].indirect(p1[:]))
+
+        for t in range(PACK):
+            size, level = [], []
+            for u in range(HALVES):
+                size.append(first_stage("w1", t, u, 3))
+                level.append(first_stage("w3", t, u, 3))
+            g = gain_sb[:, t : t + 1]
+            for u in range(HALVES):
+                cols = slice(u * BANK, (u + 1) * BANK)
+                nc.vector.scalar_tensor_tensor(
+                    out=h[t][:, cols], in0=size[u][:], scalar=g, in1=cos[t][:, cols], op0=ALU.mult, op1=ALU.mult
+                )
+            for u in range(HALVES):
+                cols = slice(u * BANK, (u + 1) * BANK)
+                nc.vector.scalar_tensor_tensor(
+                    out=h[t][:, cols], in0=level[u][:], scalar=g, in1=h[t][:, cols], op0=ALU.mult, op1=ALU.add
+                )
+            if t > 0:
+                pick_a(t - 1)
+        for u in range(2):
+            cols = slice(u * (N // 2), (u + 1) * (N // 2))
+            quantize(wa_codes[:, cols], wa_sc[:, cols], wa_bf[:, u * (2 * N) : (u + 1) * (2 * N)])
+        pick_a(PACK - 1)
+
+        x_bf, x_codes, x_sc = {}, {}, {}
+        for name in ("xa", "xb"):
+            for c in range(CHUNKS):
+                x_bf[name, c] = sb("%s_bf%d" % (name, c), [P, PACK * CHUNK], BF16)
+                x_codes[name, c] = sb("%s_codes%d" % (name, c), [P, CHUNK], U32)
+                x_sc[name, c] = sb("%s_sc%d" % (name, c), [P, CHUNK], U8)
+
+        def pick_b(c, t):
+            nc.vector.tensor_tensor(
+                xb[c][:, t, :],
+                h[t][:].indirect(p2[:, c * CHUNK // 16 : (c + 1) * CHUNK // 16]),
+                base_sb[:, t, c * CHUNK : (c + 1) * CHUNK],
+                ALU.add,
+            )
+
+        def quantize_x(name, c):
+            quantize(x_codes[name, c][:], x_sc[name, c][:], x_bf[name, c][:])
+
+        def second_stage(c):
+            for b in range(N_TILES // 2):
+                acc = psum.tile([P, 2, CHUNK], F32, name="acc_y", tag=("w1", "w3")[c], bufs=3)
+                steps = [(name, i) for name in ("xa", "xb") for i in range(2)]
+                for n, (name, i) in enumerate(steps):
+                    cols = slice((2 * b + i) * P, (2 * b + i + 1) * P)
+                    codes, scales = ((wa_codes, wa_sc), (wb_codes, wb_sc))[name == "xb"]
+                    nc.tensor.matmul_mx(
+                        out=acc[:, i, :], lhsT=codes[:, cols].bitcast(FP8X4), lhsT_scale=scales[:, cols],
+                        rhs=x_codes[name, c][:].bitcast(FP8X4), rhs_scale=x_sc[name, c][:],
+                        start=(n == 0), stop=(n == len(steps) - 1),
+                    )
+                y = sb("y%d_%d" % (c, b), [P, 2, CHUNK], F32)
+                for i in range(2):
+                    bias = bo_sb[:, 2 * b + i : 2 * b + i + 1]
+                    if c == CHUNKS - 1 and b == 1:
+                        nc.vector.tensor_scalar(out=y[:, i, :], in0=acc[:, i, :], scalar1=bias, scalar2=None, op0=ALU.add)
+                    else:
+                        nc.scalar.activation(out=y[:, i, :], in_=acc[:, i, :], func=ACT.Identity, bias=bias)
+                nc.sync.dma_start(
+                    out=out[2 * b * P : (2 * b + 2) * P, c * CHUNK : (c + 1) * CHUNK].rearrange("(i p) m -> p i m", p=P),
+                    in_=y[:],
+                )
+
+        for c in range(CHUNKS):
+            dst, src = weave_views(x_bf["xa", c][:], xa[:, :, c * CHUNK : (c + 1) * CHUNK])
+            nc.scalar.activation(out=dst, in_=src, func=ACT.Abs)
+        for t in range(PACK):
+            pick_b(0, t)
+        dst, src = weave_views(x_bf["xb", 0][:], xb[0][:])
+        nc.scalar.copy(out=dst, in_=src)
+        for c in range(CHUNKS):
+            quantize_x("xa", c)
+        for t in range(2):
+            pick_b(1, t)
+        quantize_x("xb", 0)
+        for t in range(2, PACK):
+            pick_b(1, t)
+        second_stage(0)
+        dst, src = weave_views(x_bf["xb", 1][:], xb[1][:])
+        nc.vector.tensor_copy(out=dst, in_=src)
+        quantize_x("xb", 1)
+        second_stage(1)

@@ -23,8 +23,8 @@ K_PASS = P * PACK
 PASSES = K // K_PASS
 BANK = 512
 HALVES = S // BANK
-CHUNK = 256
-CHUNKS = M // CHUNK
+WIDTHS = (256, 128, 128)
+STARTS = (0, 256, 384)
 N_TILES = N // P
 
 
@@ -43,12 +43,13 @@ def tile_list_doppler_beat_features_kernel(
         p1 = keep.tile([P, M // 16], U16, name="p1")
         p2 = keep.tile([P, M // 16], U16, name="p2")
 
-        tab_sc = sb("tab_sc", [P, T], U8)
-        v_sc = sb("v_sc", [P, S], U8)
-        v_sc1 = sb("v_sc1", [P, S], U8)
+        tab_sc = sb("tab_sc", [P, PASSES * T], U8)
+        v_sc = [sb("v_sc%d" % a, [P, S], U8) for a in range(PASSES)]
         w3_sc_raw = sb("w3_sc_raw", [P, PASSES * H], U8)
         wb_sc = sb("wb_sc", [P, N], U8)
-        for plane in (tab_sc, w3_sc_raw, v_sc1, wb_sc):
+        nc.vector.memset(tab_sc[:, 0 : 5 * T // 4].bitcast(I32), 0)
+        nc.gpsimd.memset(tab_sc[:, 5 * T // 4 : 2 * T].bitcast(I32), 0)
+        for plane in (w3_sc_raw, wb_sc):
             nc.vector.memset(plane[:].bitcast(I32), 0)
 
         def load_rows(name, rows):
@@ -62,38 +63,36 @@ def tile_list_doppler_beat_features_kernel(
             nc.sync.dma_start(out=tile[:], in_=flat)
             return tile
 
-        w2_raw = [load_rows("w2_raw%d" % a, w2[a * K_PASS : (a + 1) * K_PASS, :]) for a in range(PASSES)]
+        def load_scales(plane, rows, rs):
+            for r in rs:
+                nc.sync.dma_start(
+                    out=plane[r:P:32, :].bitcast(I32).rearrange("q (a c) -> q a c", a=rows.shape[0]),
+                    in_=rows[:, r:16:4, :].bitcast(I32).rearrange("a q c -> q a c"),
+                )
+
         nc.sync.dma_start(idx[:], offs)
-        w3_raw = sb("w3_raw", [P, PASSES, 2 * H], U8)
-        nc.sync.dma_start(out=w3_raw[:].bitcast(I32), in_=w3_words.bitcast(I32).rearrange("a p c -> p a c"))
+        w3_raw = [sb("w3_raw%d" % a, [P, 2 * H], U8) for a in range(PASSES)]
+        for a in range(PASSES):
+            nc.sync.dma_start(out=w3_raw[a][:].bitcast(I32), in_=w3_words[a].bitcast(I32))
         gain_sb = sb("gain_sb", [P, PACK], F32)
         nc.sync.dma_start(out=gain_sb[:], in_=gain.rearrange("(p t) -> p t", t=PACK))
         nc.sync.dma_start(p1[:], pos1)
         nc.sync.dma_start(p2[:], pos2)
-        tab = [load_words("tab%d" % a, tab_words[a]) for a in range(PASSES)]
+        w2_raw = [load_rows("w2_raw%d" % a, w2[a * K_PASS : (a + 1) * K_PASS, :]) for a in range(PASSES)]
+        load_scales(tab_sc, tab_scales, range(4))
+        load_scales(w3_sc_raw, w3_scales, range(2))
+        tab = [load_words("tab0", tab_words[0])]
+        load_scales(w3_sc_raw, w3_scales, range(2, 4))
+        tab.append(load_words("tab1", tab_words[1]))
         w1_raw0 = load_rows("w1_raw0", w1[0:K_PASS, :])
         w1_raw1 = [load_rows("w1_raw1_%d" % u, w1[K_PASS:K, u * (H // 2) : (u + 1) * (H // 2)]) for u in range(2)]
         wa_raw = load_rows("wa_raw", wa)
         base_sb = load_rows("base_sb", base)
         wb_codes = load_words("wb_codes", wb_words[0])
-        for q in range(4):
-            nc.sync.dma_start(
-                out=wb_sc[32 * q : 32 * q + 4, :].bitcast(I32), in_=wb_scales[0, 4 * q : 4 * q + 4, :].bitcast(I32)
-            )
+        load_scales(wb_sc, wb_scales, range(4))
         bo_sb = sb("bo_sb", [P, N_TILES], F32)
         with nc.allow_non_contiguous_dma(reason="one bias value a partition and output tile"):
             nc.sync.dma_start(out=bo_sb[:], in_=bo.rearrange("(c p) -> p c", p=P))
-
-        for q in range(4):
-            nc.gpsimd.dma_start(
-                out=tab_sc[32 * q : 32 * q + 4 * PASSES, :].bitcast(I32),
-                in_=tab_scales[:, 4 * q : 4 * q + 4, :].bitcast(I32),
-            )
-        for q in range(4):
-            nc.gpsimd.dma_start(
-                out=w3_sc_raw[32 * q : 32 * q + 4, :].bitcast(I32).rearrange("r (a c) -> r a c", a=PASSES),
-                in_=w3_scales[:, 4 * q : 4 * q + 4, :].bitcast(I32).rearrange("a r c -> r a c"),
-            )
 
         def deal(engine_copy, grouped, raw, m0):
             ms = raw.shape[2] // PACK
@@ -115,53 +114,99 @@ def tile_list_doppler_beat_features_kernel(
         w3_codes = sb("w3_codes", [P, PASSES, PACK, 2 * P], U8)
         w3_sc = sb("w3_sc", [P, PASSES, PACK, P], U8)
         for a in range(PASSES):
-            deal(nc.scalar.copy, w_bf["w2", a], w2_raw[a], 0)
-        nc.vector.tensor_copy(
-            out=w3_codes[:].rearrange("p a t (m b) -> p a t m b", b=2),
-            in_=w3_raw[:].rearrange("p a (m t b) -> p a t m b", t=PACK, b=2),
-        )
-        nc.gpsimd.tensor_copy(out=w3_sc[:], in_=w3_sc_raw[:].rearrange("p (a m t) -> p a t m", a=PASSES, t=PACK))
-        nc.vector.tensor_copy(out=v_sc[:], in_=tab_sc[:].indirect(idx[:]))
-        for q in range(4):
-            nc.gpsimd.dma_start(
-                out=v_sc1[32 * q : 32 * q + 4, :].bitcast(I32), in_=v_sc[32 * q + 4 : 32 * q + 8, :].bitcast(I32)
+            nc.vector.tensor_copy(
+                out=w3_codes[:, a, :, :].rearrange("p t (m b) -> p t m b", b=2),
+                in_=w3_raw[a][:].rearrange("p (m t b) -> p t m b", t=PACK, b=2),
             )
         for a in range(PASSES):
+            deal(nc.vector.tensor_copy, w_bf["w2", a], w2_raw[a], 0)
             quantize(w_codes["w2", a][:], w_sc["w2", a][:], w_bf["w2", a][:])
 
         v_codes = {}
         for a in range(PASSES):
+            nc.vector.tensor_copy(out=v_sc[a][:], in_=tab_sc[:, a * T : (a + 1) * T].indirect(idx[:]))
+        for a in range(PASSES):
+            if a == 1:
+                nc.vector.tensor_copy(
+                    out=w3_sc[:], in_=w3_sc_raw[:].rearrange("p (a m t) -> p a t m", a=PASSES, t=PACK)
+                )
             for u in range(HALVES):
                 v_codes[a, u] = sb("v_codes%d_%d" % (a, u), [P, BANK], U32)
                 cols = slice(u * BANK // 16, (u + 1) * BANK // 16)
                 nc.vector.tensor_copy(out=v_codes[a, u][:], in_=tab[a][:].bitcast(U32).indirect(idx[:, cols]))
 
-        def first_stage(name, t, u, bufs):
-            acc = psum.tile([P, BANK], F32, name="acc_" + name, tag=name, bufs=bufs)
+        banks = {
+            ("w2", 0, 0): 0, ("w2", 0, 1): 1, ("w3", 0, 0): 2, ("w2", 1, 0): 3, ("w2", 1, 1): 4, ("w3", 1, 0): 5,
+            ("w1", 0, 0): 6, ("w1", 0, 1): 7, ("w3", 0, 1): 0, ("w1", 1, 0): 1, ("w1", 1, 1): 2, ("w3", 1, 1): 6,
+            ("w2", 2, 0): 7, ("w2", 2, 1): 0, ("w3", 2, 0): 1, ("w1", 2, 0): 3, ("w1", 2, 1): 4, ("w3", 2, 1): 2,
+            ("w2", 3, 0): 6, ("w2", 3, 1): 7, ("w3", 3, 0): 3, ("w1", 3, 0): 5, ("w1", 3, 1): 0, ("w3", 3, 1): 4,
+        }
+
+        def first_stage(name, t, u):
+            acc = psum.tile([P, BANK], F32, name="acc_" + name, tag="bank%d" % banks[name, t, u])
             cols = slice(u * BANK, (u + 1) * BANK)
             for a in range(PASSES):
                 if name == "w3":
                     lhsT = w3_codes[:, a, t, :].bitcast(FP4X4)
                     lhsT_scale = w3_sc[:, a, t, :]
-                    rhs_scale = (v_sc, v_sc1)[a][:, cols]
                 else:
                     lhsT = w_codes[name, a][:, t * P : (t + 1) * P].bitcast(FP8X4)
                     lhsT_scale = w_sc[name, a][:, t * P : (t + 1) * P]
-                    rhs_scale = v_sc[4 * a : P, cols]
                 nc.tensor.matmul_mx(
                     out=acc[:], lhsT=lhsT, lhsT_scale=lhsT_scale, rhs=v_codes[a, u][:].bitcast(FP8X4),
-                    rhs_scale=rhs_scale, start=(a == 0), stop=(a == PASSES - 1),
+                    rhs_scale=v_sc[a][:, cols], start=(a == 0), stop=(a == PASSES - 1),
                 )
             return acc
 
+        gained = [sb("gained%d" % t, [P, BANK], F32) for t in range(PACK)]
         cos = [sb("cos%d" % t, [P, S], F32) for t in range(PACK)]
-        for t in range(PACK):
+        h = [sb("h%d" % t, [P, S], F32) for t in range(PACK)]
+        xa = sb("xa", [P, PACK, M], F32)
+        xb = [sb("xb0", [P, PACK * WIDTHS[0]], F32)[:]]
+
+        def scalar_part(t):
             folded = keep.tile([P, S], F32, name="folded", tag="scalar_stage%d" % (t % 2), align_bytes=64)
             for u in range(HALVES):
-                phase = first_stage("w2", t, u, 2)
+                phase = first_stage("w2", t, u)
                 nc.scalar.activation(out=folded[:, u * BANK : (u + 1) * BANK], in_=phase[:], func=ACT.Abs)
+            level = first_stage("w3", t, 0)
+            nc.scalar.activation(out=gained[t][:], in_=level[:], func=ACT.Copy, scale=gain_sb[:, t : t + 1])
             nc.scalar.activation(out=cos[t][:], in_=folded[:], func=ACT.Sin, bias=math.pi / 2, scale=-1.0)
 
+        def mix(t):
+            size = [first_stage("w1", t, u) for u in range(HALVES)]
+            level = first_stage("w3", t, 1)
+            g = gain_sb[:, t : t + 1]
+            for u in range(HALVES):
+                cols = slice(u * BANK, (u + 1) * BANK)
+                nc.vector.scalar_tensor_tensor(
+                    out=h[t][:, cols], in0=size[u][:], scalar=g, in1=cos[t][:, cols], op0=ALU.mult, op1=ALU.mult
+                )
+            nc.gpsimd.tensor_tensor(out=h[t][:, 0:BANK], in0=h[t][:, 0:BANK], in1=gained[t][:], op=ALU.add)
+            nc.vector.scalar_tensor_tensor(
+                out=h[t][:, BANK:S], in0=level[:], scalar=g, in1=h[t][:, BANK:S], op0=ALU.mult, op1=ALU.add
+            )
+
+        def pick_a(t):
+            nc.vector.tensor_copy(out=xa[:, t, :], in_=h[t][:].indirect(p1[:]))
+
+        def pick_b(c, t):
+            width, start = WIDTHS[c], STARTS[c]
+            nc.vector.tensor_tensor(
+                xb[c][:, t * width : (t + 1) * width],
+                h[t][:].indirect(p2[:, start // 16 : (start + width) // 16]),
+                base_sb[:, t, start : start + width],
+                ALU.add,
+            )
+
+        def weave_views(grouped, planes):
+            return (
+                grouped.rearrange("p (c i t) -> p c t i", i=4, t=PACK),
+                planes.rearrange("p t (c i) -> p c t i", i=4),
+            )
+
+        scalar_part(0)
+        scalar_part(1)
         deal(nc.vector.tensor_copy, w_bf["w1", 0], w1_raw0, 0)
         quantize(w_codes["w1", 0][:], w_sc["w1", 0][:], w_bf["w1", 0][:])
         for u in range(2):
@@ -171,107 +216,96 @@ def tile_list_doppler_beat_features_kernel(
                 w_codes["w1", 1][:, t * P : (t + 1) * P], w_sc["w1", 1][:, t * P : (t + 1) * P],
                 w_bf["w1", 1][:, t * K_PASS : (t + 1) * K_PASS],
             )
-
-        def weave_views(grouped, planes):
-            return (
-                grouped.rearrange("p (c i t) -> p c t i", i=4, t=PACK),
-                planes.rearrange("p t (c i) -> p c t i", i=4),
-            )
+        mix(0)
+        for t in range(1, PACK):
+            mix(t)
+            if t + 1 < PACK:
+                scalar_part(t + 1)
+            pick_a(t - 1)
+            pick_b(0, t - 1)
 
         wa_bf = keep.tile([P, PACK * N], BF16, name="wa_bf", tag="scalar_stage1", align_bytes=64)
         wa_codes = sb("wa_codes", [P, N], U32)
         wa_sc = sb("wa_sc", [P, N], U8)
         dst, src = weave_views(wa_bf[:], wa_raw[:])
         nc.scalar.copy(out=dst, in_=src)
-
-        h = [sb("h%d" % t, [P, S], F32) for t in range(PACK)]
-        xa = sb("xa", [P, PACK, M], F32)
-        xb = [sb("xb%d" % c, [P, PACK, CHUNK], F32) for c in range(CHUNKS)]
-
-        def pick_a(t):
-            nc.vector.tensor_copy(out=xa[:, t, :], in_=h[t][:].indirect(p1[:]))
-
-        for t in range(PACK):
-            size, level = [], []
-            for u in range(HALVES):
-                size.append(first_stage("w1", t, u, 3))
-                level.append(first_stage("w3", t, u, 3))
-            g = gain_sb[:, t : t + 1]
-            for u in range(HALVES):
-                cols = slice(u * BANK, (u + 1) * BANK)
-                nc.vector.scalar_tensor_tensor(
-                    out=h[t][:, cols], in0=size[u][:], scalar=g, in1=cos[t][:, cols], op0=ALU.mult, op1=ALU.mult
-                )
-            for u in range(HALVES):
-                cols = slice(u * BANK, (u + 1) * BANK)
-                nc.vector.scalar_tensor_tensor(
-                    out=h[t][:, cols], in0=level[u][:], scalar=g, in1=h[t][:, cols], op0=ALU.mult, op1=ALU.add
-                )
-            if t > 0:
-                pick_a(t - 1)
         for u in range(2):
             cols = slice(u * (N // 2), (u + 1) * (N // 2))
             quantize(wa_codes[:, cols], wa_sc[:, cols], wa_bf[:, u * (2 * N) : (u + 1) * (2 * N)])
         pick_a(PACK - 1)
+        pick_b(0, PACK - 1)
+        late = keep.tile([P, S], F32, name="cos%d" % (PACK - 1), align_bytes=64)
+        xb.extend([late[:, 0 : S // 2], late[:, S // 2 : S]])
+        xb_bf = [
+            late[:, S // 2 : S].bitcast(BF16),
+            late[:, 3 * S // 4 : S].bitcast(BF16),
+            sb("xb_bf2", [P, PACK * WIDTHS[2]], BF16)[:],
+        ]
+        xa_bf = sb("xa_bf", [P, PACK * M], BF16)
+        xa_codes = [sb("xa_codes%d" % u, [P, M // 2], U32) for u in range(2)]
+        xa_sc = [sb("xa_sc%d" % u, [P, M // 2], U8) for u in range(2)]
+        xb_codes = [sb("xb_codes%d" % c, [P, w], U32) for c, w in enumerate(WIDTHS)]
+        xb_sc = [sb("xb_sc%d" % c, [P, w], U8) for c, w in enumerate(WIDTHS)]
 
-        x_bf, x_codes, x_sc = {}, {}, {}
-        for name in ("xa", "xb"):
-            for c in range(CHUNKS):
-                x_bf[name, c] = sb("%s_bf%d" % (name, c), [P, PACK * CHUNK], BF16)
-                x_codes[name, c] = sb("%s_codes%d" % (name, c), [P, CHUNK], U32)
-                x_sc[name, c] = sb("%s_sc%d" % (name, c), [P, CHUNK], U8)
+        def weave_a(u):
+            dst, src = weave_views(xa_bf[:, u * 2 * M : (u + 1) * 2 * M], xa[:, :, u * M // 2 : (u + 1) * M // 2])
+            nc.scalar.activation(out=dst, in_=src, func=ACT.Abs)
 
-        def pick_b(c, t):
-            nc.vector.tensor_tensor(
-                xb[c][:, t, :],
-                h[t][:].indirect(p2[:, c * CHUNK // 16 : (c + 1) * CHUNK // 16]),
-                base_sb[:, t, c * CHUNK : (c + 1) * CHUNK],
-                ALU.add,
-            )
+        def quantize_a(u):
+            quantize(xa_codes[u][:], xa_sc[u][:], xa_bf[:, u * 2 * M : (u + 1) * 2 * M])
 
-        def quantize_x(name, c):
-            quantize(x_codes[name, c][:], x_sc[name, c][:], x_bf[name, c][:])
+        def weave_b(c, engine_copy):
+            dst, src = weave_views(xb_bf[c], xb[c].rearrange("p (t m) -> p t m", t=PACK))
+            engine_copy(out=dst, in_=src)
 
-        def second_stage(c):
-            for b in range(N_TILES // 2):
-                acc = psum.tile([P, 2, CHUNK], F32, name="acc_y", tag=("w1", "w3")[c], bufs=3)
-                steps = [(name, i) for name in ("xa", "xb") for i in range(2)]
-                for n, (name, i) in enumerate(steps):
-                    cols = slice((2 * b + i) * P, (2 * b + i + 1) * P)
-                    codes, scales = ((wa_codes, wa_sc), (wb_codes, wb_sc))[name == "xb"]
-                    nc.tensor.matmul_mx(
-                        out=acc[:, i, :], lhsT=codes[:, cols].bitcast(FP8X4), lhsT_scale=scales[:, cols],
-                        rhs=x_codes[name, c][:].bitcast(FP8X4), rhs_scale=x_sc[name, c][:],
-                        start=(n == 0), stop=(n == len(steps) - 1),
-                    )
-                y = sb("y%d_%d" % (c, b), [P, 2, CHUNK], F32)
-                for i in range(2):
-                    bias = bo_sb[:, 2 * b + i : 2 * b + i + 1]
-                    if c == CHUNKS - 1 and b == 1:
+        def quantize_b(c):
+            quantize(xb_codes[c][:], xb_sc[c][:], xb_bf[c])
+
+        def second_stage(c, bank_numbers):
+            width, start = WIDTHS[c], STARTS[c]
+            tiles = N_TILES // len(bank_numbers)
+            u, within = divmod(start, M // 2)
+            a_cols = slice(within, within + width)
+            operands = [
+                (wa_codes, wa_sc, xa_codes[u][:, a_cols], xa_sc[u][:, a_cols]),
+                (wb_codes, wb_sc, xb_codes[c][:], xb_sc[c][:]),
+            ]
+            for b, number in enumerate(bank_numbers):
+                acc = psum.tile([P, tiles, width], F32, name="acc_y", tag="bank%d" % number)
+                for n, (codes, scales, x_codes, x_scales) in enumerate(operands):
+                    for i in range(tiles):
+                        cols = slice((tiles * b + i) * P, (tiles * b + i + 1) * P)
+                        nc.tensor.matmul_mx(
+                            out=acc[:, i, :], lhsT=codes[:, cols].bitcast(FP8X4), lhsT_scale=scales[:, cols],
+                            rhs=x_codes.bitcast(FP8X4), rhs_scale=x_scales,
+                            start=(n == 0 and i == 0), stop=(n == 1 and i == tiles - 1),
+                        )
+                y = sb("y%d_%d" % (c, b), [P, tiles, width], F32)
+                for i in range(tiles):
+                    bias = bo_sb[:, tiles * b + i : tiles * b + i + 1]
+                    if c == len(WIDTHS) - 1 and b == 1:
                         nc.vector.tensor_scalar(out=y[:, i, :], in0=acc[:, i, :], scalar1=bias, scalar2=None, op0=ALU.add)
                     else:
                         nc.scalar.activation(out=y[:, i, :], in_=acc[:, i, :], func=ACT.Identity, bias=bias)
-                nc.sync.dma_start(
-                    out=out[2 * b * P : (2 * b + 2) * P, c * CHUNK : (c + 1) * CHUNK].rearrange("(i p) m -> p i m", p=P),
-                    in_=y[:],
-                )
+                rows = out[tiles * b * P : tiles * (b + 1) * P, start : start + width]
+                nc.sync.dma_start(out=rows.rearrange("(i p) m -> p i m", p=P), in_=y[:])
 
-        for c in range(CHUNKS):
-            dst, src = weave_views(x_bf["xa", c][:], xa[:, :, c * CHUNK : (c + 1) * CHUNK])
-            nc.scalar.activation(out=dst, in_=src, func=ACT.Abs)
+        weave_a(0)
+        weave_b(0, nc.scalar.copy)
+        weave_a(1)
         for t in range(PACK):
-            pick_b(0, t)
-        dst, src = weave_views(x_bf["xb", 0][:], xb[0][:])
-        nc.scalar.copy(out=dst, in_=src)
-        for c in range(CHUNKS):
-            quantize_x("xa", c)
+            pick_b(1, t)
+        quantize_a(0)
+        quantize_b(0)
+        weave_b(1, nc.scalar.copy)
+        second_stage(0, (1, 2, 3))
         for t in range(2):
-            pick_b(1, t)
-        quantize_x("xb", 0)
+            pick_b(2, t)
+        quantize_a(1)
+        quantize_b(1)
+        second_stage(1, (5, 6))
         for t in range(2, PACK):
-            pick_b(1, t)
-        second_stage(0)
-        dst, src = weave_views(x_bf["xb", 1][:], xb[1][:])
-        nc.vector.tensor_copy(out=dst, in_=src)
-        quantize_x("xb", 1)
-        second_stage(1)
+            pick_b(2, t)
+        weave_b(2, nc.vector.tensor_copy)
+        quantize_b(2)
+        second_stage(2, (7, 0))

@@ -23,9 +23,25 @@ K_PASS = P * PACK
 PASSES = K // K_PASS
 BANK = 512
 HALVES = S // BANK
+PER_COLUMN = 16
+QUADRANT = 32
+SCALE_ROWS = 4
+LINE = 4
+N_TILES = N // P
+
 WIDTHS = (256, 128, 128)
 STARTS = (0, 256, 384)
-N_TILES = N // P
+
+VECTOR_CLEARS = 5 * PASSES * T // 8
+
+BANKS = {
+    ("w2", 0, 0): 0, ("w2", 0, 1): 1, ("w3", 0, 0): 2, ("w2", 1, 0): 3, ("w2", 1, 1): 4, ("w3", 1, 0): 5,
+    ("w1", 0, 0): 6, ("w1", 0, 1): 7, ("w1", 1, 0): 1, ("w3", 0, 1): 0, ("w1", 1, 1): 2,
+    ("w2", 2, 0): 7, ("w2", 2, 1): 0, ("w3", 2, 0): 1, ("w1", 2, 0): 3, ("w3", 1, 1): 6, ("w1", 2, 1): 4,
+    ("w2", 3, 0): 7, ("w2", 3, 1): 6, ("w3", 3, 0): 3, ("w1", 3, 0): 5, ("w3", 2, 1): 2, ("w1", 3, 1): 0,
+    ("w3", 3, 1): 4,
+}
+OUT_BANKS = ((1, 2, 3), (5, 6), (7, 0))
 
 
 def tile_list_doppler_beat_features_kernel(
@@ -36,19 +52,19 @@ def tile_list_doppler_beat_features_kernel(
         keep = ctx.enter_context(tc.tile_pool(name="keep", bufs=1))
         psum = ctx.enter_context(tc.psum_pool(name="psum", bufs=1))
 
-        def sb(name, shape, dtype):
-            return keep.tile(shape, dtype, name=name, align_bytes=64)
+        def sb(name, shape, dtype, tag=None):
+            return keep.tile(shape, dtype, name=name, tag=tag or name, align_bytes=64)
 
-        idx = keep.tile([P, S // 16], U16, name="idx")
-        p1 = keep.tile([P, M // 16], U16, name="p1")
-        p2 = keep.tile([P, M // 16], U16, name="p2")
+        idx = keep.tile([P, S // PER_COLUMN], U16, name="idx")
+        p1 = keep.tile([P, M // PER_COLUMN], U16, name="p1")
+        p2 = keep.tile([P, M // PER_COLUMN], U16, name="p2")
 
         tab_sc = sb("tab_sc", [P, PASSES * T], U8)
         v_sc = [sb("v_sc%d" % a, [P, S], U8) for a in range(PASSES)]
         w3_sc_raw = sb("w3_sc_raw", [P, PASSES * H], U8)
         wb_sc = sb("wb_sc", [P, N], U8)
-        nc.vector.memset(tab_sc[:, 0 : 5 * T // 4].bitcast(I32), 0)
-        nc.gpsimd.memset(tab_sc[:, 5 * T // 4 : 2 * T].bitcast(I32), 0)
+        nc.vector.memset(tab_sc[:, 0:VECTOR_CLEARS].bitcast(I32), 0)
+        nc.gpsimd.memset(tab_sc[:, VECTOR_CLEARS : PASSES * T].bitcast(I32), 0)
         for plane in (w3_sc_raw, wb_sc):
             nc.vector.memset(plane[:].bitcast(I32), 0)
 
@@ -63,11 +79,11 @@ def tile_list_doppler_beat_features_kernel(
             nc.sync.dma_start(out=tile[:], in_=flat)
             return tile
 
-        def load_scales(plane, rows, rs):
-            for r in rs:
+        def load_scales(planes, rows, places):
+            for place in places:
                 nc.sync.dma_start(
-                    out=plane[r:P:32, :].bitcast(I32).rearrange("q (a c) -> q a c", a=rows.shape[0]),
-                    in_=rows[:, r:16:4, :].bitcast(I32).rearrange("a q c -> q a c"),
+                    out=planes[place:P:QUADRANT, :].bitcast(I32).rearrange("q (a c) -> q a c", a=rows.shape[0]),
+                    in_=rows[:, place : P // 8 : SCALE_ROWS, :].bitcast(I32).rearrange("a q c -> q a c"),
                 )
 
         nc.sync.dma_start(idx[:], offs)
@@ -79,25 +95,25 @@ def tile_list_doppler_beat_features_kernel(
         nc.sync.dma_start(p1[:], pos1)
         nc.sync.dma_start(p2[:], pos2)
         w2_raw = [load_rows("w2_raw%d" % a, w2[a * K_PASS : (a + 1) * K_PASS, :]) for a in range(PASSES)]
-        load_scales(tab_sc, tab_scales, range(4))
-        load_scales(w3_sc_raw, w3_scales, range(2))
+        load_scales(tab_sc, tab_scales, range(SCALE_ROWS))
+        load_scales(w3_sc_raw, w3_scales, range(SCALE_ROWS // 2))
         tab = [load_words("tab0", tab_words[0])]
-        load_scales(w3_sc_raw, w3_scales, range(2, 4))
+        load_scales(w3_sc_raw, w3_scales, range(SCALE_ROWS // 2, SCALE_ROWS))
         tab.append(load_words("tab1", tab_words[1]))
-        w1_raw0 = load_rows("w1_raw0", w1[0:K_PASS, :])
-        w1_raw1 = [load_rows("w1_raw1_%d" % u, w1[K_PASS:K, u * (H // 2) : (u + 1) * (H // 2)]) for u in range(2)]
+        w1_first = load_rows("w1_first", w1[0:K_PASS, :])
+        w1_last = [load_rows("w1_last%d" % u, w1[K_PASS:K, u * (H // 2) : (u + 1) * (H // 2)]) for u in range(2)]
         wa_raw = load_rows("wa_raw", wa)
         base_sb = load_rows("base_sb", base)
         wb_codes = load_words("wb_codes", wb_words[0])
-        load_scales(wb_sc, wb_scales, range(4))
+        load_scales(wb_sc, wb_scales, range(SCALE_ROWS))
         bo_sb = sb("bo_sb", [P, N_TILES], F32)
-        with nc.allow_non_contiguous_dma(reason="one bias value a partition and output tile"):
+        with nc.allow_non_contiguous_dma(reason="one bias value for each partition and output tile"):
             nc.sync.dma_start(out=bo_sb[:], in_=bo.rearrange("(c p) -> p c", p=P))
 
-        def deal(engine_copy, grouped, raw, m0):
-            ms = raw.shape[2] // PACK
-            engine_copy(
-                out=grouped[:].rearrange("p (t m j) -> p m t j", t=PACK, j=PACK)[:, m0 : m0 + ms, :, :],
+        def deal(grouped, raw, m0):
+            count = raw.shape[2] // PACK
+            nc.vector.tensor_copy(
+                out=grouped[:].rearrange("p (t m j) -> p m t j", t=PACK, j=PACK)[:, m0 : m0 + count, :, :],
                 in_=raw[:].rearrange("p j (m t) -> p m t j", t=PACK),
             )
 
@@ -119,31 +135,25 @@ def tile_list_doppler_beat_features_kernel(
                 in_=w3_raw[a][:].rearrange("p (m t b) -> p t m b", t=PACK, b=2),
             )
         for a in range(PASSES):
-            deal(nc.vector.tensor_copy, w_bf["w2", a], w2_raw[a], 0)
+            deal(w_bf["w2", a], w2_raw[a], 0)
             quantize(w_codes["w2", a][:], w_sc["w2", a][:], w_bf["w2", a][:])
 
         v_codes = {}
-        for a in range(PASSES):
-            nc.vector.tensor_copy(out=v_sc[a][:], in_=tab_sc[:, a * T : (a + 1) * T].indirect(idx[:]))
-        for a in range(PASSES):
-            if a == 1:
-                nc.vector.tensor_copy(
-                    out=w3_sc[:], in_=w3_sc_raw[:].rearrange("p (a m t) -> p a t m", a=PASSES, t=PACK)
-                )
+
+        def gather_words(a):
             for u in range(HALVES):
                 v_codes[a, u] = sb("v_codes%d_%d" % (a, u), [P, BANK], U32)
-                cols = slice(u * BANK // 16, (u + 1) * BANK // 16)
-                nc.vector.tensor_copy(out=v_codes[a, u][:], in_=tab[a][:].bitcast(U32).indirect(idx[:, cols]))
+                entries = idx[:, u * BANK // PER_COLUMN : (u + 1) * BANK // PER_COLUMN]
+                nc.vector.tensor_copy(out=v_codes[a, u][:], in_=tab[a][:].bitcast(U32).indirect(entries))
 
-        banks = {
-            ("w2", 0, 0): 0, ("w2", 0, 1): 1, ("w3", 0, 0): 2, ("w2", 1, 0): 3, ("w2", 1, 1): 4, ("w3", 1, 0): 5,
-            ("w1", 0, 0): 6, ("w1", 0, 1): 7, ("w3", 0, 1): 0, ("w1", 1, 0): 1, ("w1", 1, 1): 2, ("w3", 1, 1): 6,
-            ("w2", 2, 0): 7, ("w2", 2, 1): 0, ("w3", 2, 0): 1, ("w1", 2, 0): 3, ("w1", 2, 1): 4, ("w3", 2, 1): 2,
-            ("w2", 3, 0): 6, ("w2", 3, 1): 7, ("w3", 3, 0): 3, ("w1", 3, 0): 5, ("w1", 3, 1): 0, ("w3", 3, 1): 4,
-        }
+        for a in range(PASSES):
+            nc.vector.tensor_copy(out=v_sc[a][:], in_=tab_sc[:, a * T : (a + 1) * T].indirect(idx[:]))
+        gather_words(0)
+        nc.vector.tensor_copy(out=w3_sc[:], in_=w3_sc_raw[:].rearrange("p (a m t) -> p a t m", a=PASSES, t=PACK))
+        gather_words(1)
 
         def first_stage(name, t, u):
-            acc = psum.tile([P, BANK], F32, name="acc_" + name, tag="bank%d" % banks[name, t, u])
+            acc = psum.tile([P, BANK], F32, name="acc_" + name, tag="bank%d" % BANKS[name, t, u])
             cols = slice(u * BANK, (u + 1) * BANK)
             for a in range(PASSES):
                 if name == "w3":
@@ -165,26 +175,32 @@ def tile_list_doppler_beat_features_kernel(
         xb = [sb("xb0", [P, PACK * WIDTHS[0]], F32)[:]]
 
         def scalar_part(t):
-            folded = keep.tile([P, S], F32, name="folded", tag="scalar_stage%d" % (t % 2), align_bytes=64)
+            folded = sb("folded", [P, S], F32, tag="scalar_stage%d" % (t % 2))
             for u in range(HALVES):
                 phase = first_stage("w2", t, u)
                 nc.scalar.activation(out=folded[:, u * BANK : (u + 1) * BANK], in_=phase[:], func=ACT.Abs)
             level = first_stage("w3", t, 0)
             nc.scalar.activation(out=gained[t][:], in_=level[:], func=ACT.Copy, scale=gain_sb[:, t : t + 1])
-            nc.scalar.activation(out=cos[t][:], in_=folded[:], func=ACT.Sin, bias=math.pi / 2, scale=-1.0)
-
-        def mix(t):
-            size = [first_stage("w1", t, u) for u in range(HALVES)]
-            level = first_stage("w3", t, 1)
-            g = gain_sb[:, t : t + 1]
             for u in range(HALVES):
                 cols = slice(u * BANK, (u + 1) * BANK)
-                nc.vector.scalar_tensor_tensor(
-                    out=h[t][:, cols], in0=size[u][:], scalar=g, in1=cos[t][:, cols], op0=ALU.mult, op1=ALU.mult
-                )
-            nc.gpsimd.tensor_tensor(out=h[t][:, 0:BANK], in0=h[t][:, 0:BANK], in1=gained[t][:], op=ALU.add)
+                nc.scalar.activation(out=cos[t][:, cols], in_=folded[:, cols], func=ACT.Sin, bias=math.pi / 2, scale=-1.0)
+
+        def modulate(t, u):
+            size = first_stage("w1", t, u)
+            cols = slice(u * BANK, (u + 1) * BANK)
             nc.vector.scalar_tensor_tensor(
-                out=h[t][:, BANK:S], in0=level[:], scalar=g, in1=h[t][:, BANK:S], op0=ALU.mult, op1=ALU.add
+                out=h[t][:, cols], in0=size[:], scalar=gain_sb[:, t : t + 1], in1=cos[t][:, cols],
+                op0=ALU.mult, op1=ALU.mult,
+            )
+
+        def add_level_first_half(t):
+            nc.gpsimd.tensor_tensor(out=h[t][:, 0:BANK], in0=h[t][:, 0:BANK], in1=gained[t][:], op=ALU.add)
+
+        def add_level_second_half(t):
+            level = first_stage("w3", t, 1)
+            nc.vector.scalar_tensor_tensor(
+                out=h[t][:, BANK:S], in0=level[:], scalar=gain_sb[:, t : t + 1], in1=h[t][:, BANK:S],
+                op0=ALU.mult, op1=ALU.add,
             )
 
         def pick_a(t):
@@ -194,47 +210,57 @@ def tile_list_doppler_beat_features_kernel(
             width, start = WIDTHS[c], STARTS[c]
             nc.vector.tensor_tensor(
                 xb[c][:, t * width : (t + 1) * width],
-                h[t][:].indirect(p2[:, start // 16 : (start + width) // 16]),
+                h[t][:].indirect(p2[:, start // PER_COLUMN : (start + width) // PER_COLUMN]),
                 base_sb[:, t, start : start + width],
                 ALU.add,
             )
 
-        def weave_views(grouped, planes):
+        def weave_views(grouped, rows):
             return (
-                grouped.rearrange("p (c i t) -> p c t i", i=4, t=PACK),
-                planes.rearrange("p t (c i) -> p c t i", i=4),
+                grouped.rearrange("p (c i t) -> p c t i", i=LINE, t=PACK),
+                rows.rearrange("p t (c i) -> p c t i", i=LINE),
             )
 
         scalar_part(0)
         scalar_part(1)
-        deal(nc.vector.tensor_copy, w_bf["w1", 0], w1_raw0, 0)
+        deal(w_bf["w1", 0], w1_first, 0)
         quantize(w_codes["w1", 0][:], w_sc["w1", 0][:], w_bf["w1", 0][:])
         for u in range(2):
-            deal(nc.vector.tensor_copy, w_bf["w1", 1], w1_raw1[u], u * (P // 2))
+            deal(w_bf["w1", 1], w1_last[u], u * (P // 2))
         for t in range(PACK):
             quantize(
                 w_codes["w1", 1][:, t * P : (t + 1) * P], w_sc["w1", 1][:, t * P : (t + 1) * P],
                 w_bf["w1", 1][:, t * K_PASS : (t + 1) * K_PASS],
             )
-        mix(0)
+
+        last = PACK - 1
+        modulate(0, 0)
+        add_level_first_half(0)
+        modulate(0, 1)
         for t in range(1, PACK):
-            mix(t)
-            if t + 1 < PACK:
+            modulate(t, 0)
+            add_level_first_half(t)
+            add_level_second_half(t - 1)
+            modulate(t, 1)
+            if t < last:
                 scalar_part(t + 1)
             pick_a(t - 1)
+            if t == last:
+                add_level_second_half(last)
             pick_b(0, t - 1)
+        pick_a(last)
+        pick_b(0, last)
 
-        wa_bf = keep.tile([P, PACK * N], BF16, name="wa_bf", tag="scalar_stage1", align_bytes=64)
         wa_codes = sb("wa_codes", [P, N], U32)
         wa_sc = sb("wa_sc", [P, N], U8)
+        wa_bf = sb("wa_bf", [P, PACK * N], BF16, tag="scalar_stage%d" % (last % 2))
         dst, src = weave_views(wa_bf[:], wa_raw[:])
         nc.scalar.copy(out=dst, in_=src)
         for u in range(2):
             cols = slice(u * (N // 2), (u + 1) * (N // 2))
             quantize(wa_codes[:, cols], wa_sc[:, cols], wa_bf[:, u * (2 * N) : (u + 1) * (2 * N)])
-        pick_a(PACK - 1)
-        pick_b(0, PACK - 1)
-        late = keep.tile([P, S], F32, name="cos%d" % (PACK - 1), align_bytes=64)
+
+        late = sb("late", [P, S], F32, tag="cos%d" % last)
         xb.extend([late[:, 0 : S // 2], late[:, S // 2 : S]])
         xb_bf = [
             late[:, S // 2 : S].bitcast(BF16),
@@ -261,16 +287,16 @@ def tile_list_doppler_beat_features_kernel(
         def quantize_b(c):
             quantize(xb_codes[c][:], xb_sc[c][:], xb_bf[c])
 
-        def second_stage(c, bank_numbers):
+        def second_stage(c):
             width, start = WIDTHS[c], STARTS[c]
-            tiles = N_TILES // len(bank_numbers)
+            tiles = N_TILES // len(OUT_BANKS[c])
             u, within = divmod(start, M // 2)
             a_cols = slice(within, within + width)
             operands = [
                 (wa_codes, wa_sc, xa_codes[u][:, a_cols], xa_sc[u][:, a_cols]),
                 (wb_codes, wb_sc, xb_codes[c][:], xb_sc[c][:]),
             ]
-            for b, number in enumerate(bank_numbers):
+            for b, number in enumerate(OUT_BANKS[c]):
                 acc = psum.tile([P, tiles, width], F32, name="acc_y", tag="bank%d" % number)
                 for n, (codes, scales, x_codes, x_scales) in enumerate(operands):
                     for i in range(tiles):
@@ -281,9 +307,10 @@ def tile_list_doppler_beat_features_kernel(
                             start=(n == 0 and i == 0), stop=(n == 1 and i == tiles - 1),
                         )
                 y = sb("y%d_%d" % (c, b), [P, tiles, width], F32)
+                vector_is_free = c == len(WIDTHS) - 1 and b == 1
                 for i in range(tiles):
                     bias = bo_sb[:, tiles * b + i : tiles * b + i + 1]
-                    if c == len(WIDTHS) - 1 and b == 1:
+                    if vector_is_free:
                         nc.vector.tensor_scalar(out=y[:, i, :], in0=acc[:, i, :], scalar1=bias, scalar2=None, op0=ALU.add)
                     else:
                         nc.scalar.activation(out=y[:, i, :], in_=acc[:, i, :], func=ACT.Identity, bias=bias)
@@ -298,14 +325,14 @@ def tile_list_doppler_beat_features_kernel(
         quantize_a(0)
         quantize_b(0)
         weave_b(1, nc.scalar.copy)
-        second_stage(0, (1, 2, 3))
-        for t in range(2):
+        second_stage(0)
+        for t in range(PACK // 2):
             pick_b(2, t)
         quantize_a(1)
         quantize_b(1)
-        second_stage(1, (5, 6))
-        for t in range(2, PACK):
+        second_stage(1)
+        for t in range(PACK // 2, PACK):
             pick_b(2, t)
         weave_b(2, nc.vector.tensor_copy)
         quantize_b(2)
-        second_stage(2, (7, 0))
+        second_stage(2)

import math
from contextlib import ExitStack

import concourse.mybir as mybir

K, T, S, H, M, N = 1024, 4096, 1024, 512, 512, 768
FLOPS = 2 * (3 * K * H * S + 2 * H * N * M)

F32 = mybir.dt.float32
BF16 = mybir.dt.bfloat16
I32 = mybir.dt.int32
U32 = mybir.dt.uint32
U16 = mybir.dt.uint16
U8 = mybir.dt.uint8
FP8X4 = mybir.dt.float8_e4m3fn_x4
FP4X4 = mybir.dt.float4_e2m1fn_x4
ALU = mybir.AluOpType
ACT = mybir.ActivationFunctionType

P = 128
PACK = 4
K_PASS = P * PACK
PASSES = K // K_PASS
BANK = 512
HALVES = S // BANK
PER_COLUMN = 16
QUADRANT = 32
SCALE_ROWS = 4
LINE = 4
N_TILES = N // P

WIDTHS = (256, 128, 128)
STARTS = (0, 256, 384)

VECTOR_CLEARS = 5 * PASSES * T // 8

BANKS = {
    ("w2", 0, 0): 0, ("w2", 0, 1): 1, ("w3", 0, 0): 2, ("w2", 1, 0): 3, ("w2", 1, 1): 4, ("w3", 1, 0): 5,
    ("w1", 0, 0): 6, ("w1", 0, 1): 7, ("w1", 1, 0): 1, ("w3", 0, 1): 0, ("w1", 1, 1): 2,
    ("w2", 2, 0): 7, ("w2", 2, 1): 0, ("w3", 2, 0): 1, ("w1", 2, 0): 3, ("w3", 1, 1): 6, ("w1", 2, 1): 4,
    ("w2", 3, 0): 7, ("w2", 3, 1): 6, ("w3", 3, 0): 3, ("w1", 3, 0): 5, ("w3", 2, 1): 2, ("w1", 3, 1): 0,
    ("w3", 3, 1): 4,
}
OUT_BANKS = ((1, 2, 3), (5, 6), (7, 0))


def tile_list_doppler_beat_features_kernel(
    tc, tab_words, tab_scales, offs, pos1, pos2, w1, w2, w3_words, w3_scales, gain, base, wa, wb_words, wb_scales, bo, out
):
    nc = tc.nc
    with ExitStack() as ctx:
        keep = ctx.enter_context(tc.tile_pool(name="keep", bufs=1))
        psum = ctx.enter_context(tc.psum_pool(name="psum", bufs=1))

        def sb(name, shape, dtype, tag=None):
            return keep.tile(shape, dtype, name=name, tag=tag or name, align_bytes=64)

        idx = keep.tile([P, S // PER_COLUMN], U16, name="idx")
        p1 = keep.tile([P, M // PER_COLUMN], U16, name="p1")
        p2 = keep.tile([P, M // PER_COLUMN], U16, name="p2")

        tab_sc = sb("tab_sc", [P, PASSES * T], U8)
        v_sc = [sb("v_sc%d" % a, [P, S], U8) for a in range(PASSES)]
        w3_sc_raw = sb("w3_sc_raw", [P, PASSES * H], U8)
        wb_sc = sb("wb_sc", [P, N], U8)
        nc.vector.memset(tab_sc[:, 0:VECTOR_CLEARS].bitcast(I32), 0)
        nc.gpsimd.memset(tab_sc[:, VECTOR_CLEARS : PASSES * T].bitcast(I32), 0)
        for plane in (w3_sc_raw, wb_sc):
            nc.vector.memset(plane[:].bitcast(I32), 0)

        def load_rows(name, rows):
            raw = sb(name, [P, PACK, rows.shape[1]], F32)
            nc.sync.dma_start(out=raw[:], in_=rows.rearrange("(p j) w -> p j w", j=PACK))
            return raw

        def load_words(name, words):
            flat = words.rearrange("p t i -> p (t i)").bitcast(I32)
            tile = sb(name, [P, flat.shape[1]], I32)
            nc.sync.dma_start(out=tile[:], in_=flat)
            return tile

        def load_scales(planes, rows, places):
            for place in places:
                nc.sync.dma_start(
                    out=planes[place:P:QUADRANT, :].bitcast(I32).rearrange("q (a c) -> q a c", a=rows.shape[0]),
                    in_=rows[:, place : P // 8 : SCALE_ROWS, :].bitcast(I32).rearrange("a q c -> q a c"),
                )

        nc.sync.dma_start(idx[:], offs)
        w3_raw = [sb("w3_raw%d" % a, [P, 2 * H], U8) for a in range(PASSES)]
        for a in range(PASSES):
            nc.sync.dma_start(out=w3_raw[a][:].bitcast(I32), in_=w3_words[a].bitcast(I32))
        gain_sb = sb("gain_sb", [P, PACK], F32)
        nc.sync.dma_start(out=gain_sb[:], in_=gain.rearrange("(p t) -> p t", t=PACK))
        nc.sync.dma_start(p1[:], pos1)
        nc.sync.dma_start(p2[:], pos2)
        w2_raw = [load_rows("w2_raw%d" % a, w2[a * K_PASS : (a + 1) * K_PASS, :]) for a in range(PASSES)]
        load_scales(tab_sc, tab_scales, range(SCALE_ROWS))
        load_scales(w3_sc_raw, w3_scales, range(SCALE_ROWS // 2))
        tab = [load_words("tab0", tab_words[0])]
        load_scales(w3_sc_raw, w3_scales, range(SCALE_ROWS // 2, SCALE_ROWS))
        tab.append(load_words("tab1", tab_words[1]))
        w1_first = load_rows("w1_first", w1[0:K_PASS, :])
        w1_last = [load_rows("w1_last%d" % u, w1[K_PASS:K, u * (H // 2) : (u + 1) * (H // 2)]) for u in range(2)]
        wa_raw = load_rows("wa_raw", wa)
        base_sb = load_rows("base_sb", base)
        wb_codes = load_words("wb_codes", wb_words[0])
        load_scales(wb_sc, wb_scales, range(SCALE_ROWS))
        bo_sb = sb("bo_sb", [P, N_TILES], F32)
        with nc.allow_non_contiguous_dma(reason="one bias value for each partition and output tile"):
            nc.sync.dma_start(out=bo_sb[:], in_=bo.rearrange("(c p) -> p c", p=P))

        def deal(grouped, raw, m0):
            count = raw.shape[2] // PACK
            nc.vector.tensor_copy(
                out=grouped[:].rearrange("p (t m j) -> p m t j", t=PACK, j=PACK)[:, m0 : m0 + count, :, :],
                in_=raw[:].rearrange("p j (m t) -> p m t j", t=PACK),
            )

        def quantize(codes, scales, grouped):
            nc.vector.quantize_mx(out=codes.bitcast(FP8X4), scales=scales, in_=grouped)

        w_codes, w_sc, w_bf = {}, {}, {}
        for name in ("w1", "w2"):
            for a in range(PASSES):
                w_codes[name, a] = sb("%s_codes%d" % (name, a), [P, H], U32)
                w_sc[name, a] = sb("%s_sc%d" % (name, a), [P, H], U8)
                w_bf[name, a] = sb("%s_bf%d" % (name, a), [P, PACK * H], BF16)

        w3_codes = sb("w3_codes", [P, PASSES, PACK, 2 * P], U8)
        w3_sc = sb("w3_sc", [P, PASSES, PACK, P], U8)
        for a in range(PASSES):
            nc.vector.tensor_copy(
                out=w3_codes[:, a, :, :].rearrange("p t (m b) -> p t m b", b=2),
                in_=w3_raw[a][:].rearrange("p (m t b) -> p t m b", t=PACK, b=2),
            )
        for a in range(PASSES):
            deal(w_bf["w2", a], w2_raw[a], 0)
            quantize(w_codes["w2", a][:], w_sc["w2", a][:], w_bf["w2", a][:])

        v_codes = {}

        def gather_words(a):
            for u in range(HALVES):
                v_codes[a, u] = sb("v_codes%d_%d" % (a, u), [P, BANK], U32)
                entries = idx[:, u * BANK // PER_COLUMN : (u + 1) * BANK // PER_COLUMN]
                nc.vector.tensor_copy(out=v_codes[a, u][:], in_=tab[a][:].bitcast(U32).indirect(entries))

        for a in range(PASSES):
            nc.vector.tensor_copy(out=v_sc[a][:], in_=tab_sc[:, a * T : (a + 1) * T].indirect(idx[:]))
        gather_words(0)
        nc.vector.tensor_copy(out=w3_sc[:], in_=w3_sc_raw[:].rearrange("p (a m t) -> p a t m", a=PASSES, t=PACK))
        gather_words(1)

        def first_stage(name, t, u):
            acc = psum.tile([P, BANK], F32, name="acc_" + name, tag="bank%d" % BANKS[name, t, u])
            cols = slice(u * BANK, (u + 1) * BANK)
            for a in range(PASSES):
                if name == "w3":
                    lhsT = w3_codes[:, a, t, :].bitcast(FP4X4)
                    lhsT_scale = w3_sc[:, a, t, :]
                else:
                    lhsT = w_codes[name, a][:, t * P : (t + 1) * P].bitcast(FP8X4)
                    lhsT_scale = w_sc[name, a][:, t * P : (t + 1) * P]
                nc.tensor.matmul_mx(
                    out=acc[:], lhsT=lhsT, lhsT_scale=lhsT_scale, rhs=v_codes[a, u][:].bitcast(FP8X4),
                    rhs_scale=v_sc[a][:, cols], start=(a == 0), stop=(a == PASSES - 1),
                )
            return acc

        gained = [sb("gained%d" % t, [P, BANK], F32) for t in range(PACK)]
        cos = [sb("cos%d" % t, [P, S], F32) for t in range(PACK)]
        h = [sb("h%d" % t, [P, S], F32) for t in range(PACK)]
        xa = sb("xa", [P, PACK, M], F32)
        xb = [sb("xb0", [P, PACK * WIDTHS[0]], F32)[:]]

        def scalar_part(t):
            folded = sb("folded", [P, S], F32, tag="scalar_stage%d" % (t % 2))
            for u in range(HALVES):
                phase = first_stage("w2", t, u)
                nc.scalar.activation(out=folded[:, u * BANK : (u + 1) * BANK], in_=phase[:], func=ACT.Abs)
            level = first_stage("w3", t, 0)
            nc.scalar.activation(out=gained[t][:], in_=level[:], func=ACT.Copy, scale=gain_sb[:, t : t + 1])
            for u in range(HALVES):
                cols = slice(u * BANK, (u + 1) * BANK)
                nc.scalar.activation(out=cos[t][:, cols], in_=folded[:, cols], func=ACT.Sin, bias=math.pi / 2, scale=-1.0)

        def modulate(t, u):
            size = first_stage("w1", t, u)
            cols = slice(u * BANK, (u + 1) * BANK)
            nc.vector.scalar_tensor_tensor(
                out=h[t][:, cols], in0=size[:], scalar=gain_sb[:, t : t + 1], in1=cos[t][:, cols],
                op0=ALU.mult, op1=ALU.mult,
            )

        def add_level_first_half(t):
            nc.gpsimd.tensor_tensor(out=h[t][:, 0:BANK], in0=h[t][:, 0:BANK], in1=gained[t][:], op=ALU.add)

        def add_level_second_half(t):
            level = first_stage("w3", t, 1)
            nc.vector.scalar_tensor_tensor(
                out=h[t][:, BANK:S], in0=level[:], scalar=gain_sb[:, t : t + 1], in1=h[t][:, BANK:S],
                op0=ALU.mult, op1=ALU.add,
            )

        def pick_a(t):
            nc.vector.tensor_copy(out=xa[:, t, :], in_=h[t][:].indirect(p1[:]))

        def pick_b(c, t):
            width, start = WIDTHS[c], STARTS[c]
            nc.vector.tensor_tensor(
                xb[c][:, t * width : (t + 1) * width],
                h[t][:].indirect(p2[:, start // PER_COLUMN : (start + width) // PER_COLUMN]),
                base_sb[:, t, start : start + width],
                ALU.add,
            )

        def weave_views(grouped, rows):
            return (
                grouped.rearrange("p (c i t) -> p c t i", i=LINE, t=PACK),
                rows.rearrange("p t (c i) -> p c t i", i=LINE),
            )

        scalar_part(0)
        scalar_part(1)
        deal(w_bf["w1", 0], w1_first, 0)
        quantize(w_codes["w1", 0][:], w_sc["w1", 0][:], w_bf["w1", 0][:])
        for u in range(2):
            deal(w_bf["w1", 1], w1_last[u], u * (P // 2))
        for t in range(PACK):
            quantize(
                w_codes["w1", 1][:, t * P : (t + 1) * P], w_sc["w1", 1][:, t * P : (t + 1) * P],
                w_bf["w1", 1][:, t * K_PASS : (t + 1) * K_PASS],
            )

        last = PACK - 1
        modulate(0, 0)
        add_level_first_half(0)
        modulate(0, 1)
        for t in range(1, PACK):
            modulate(t, 0)
            add_level_first_half(t)
            add_level_second_half(t - 1)
            modulate(t, 1)
            if t < last:
                scalar_part(t + 1)
            pick_a(t - 1)
            if t == last:
                add_level_second_half(last)
            pick_b(0, t - 1)
        pick_a(last)
        pick_b(0, last)

        wa_codes = sb("wa_codes", [P, N], U32)
        wa_sc = sb("wa_sc", [P, N], U8)
        wa_bf = sb("wa_bf", [P, PACK * N], BF16, tag="scalar_stage%d" % (last % 2))
        dst, src = weave_views(wa_bf[:], wa_raw[:])
        nc.scalar.copy(out=dst, in_=src)
        for u in range(2):
            cols = slice(u * (N // 2), (u + 1) * (N // 2))
            quantize(wa_codes[:, cols], wa_sc[:, cols], wa_bf[:, u * (2 * N) : (u + 1) * (2 * N)])

        late = sb("late", [P, S], F32, tag="cos%d" % last)
        xb.extend([late[:, 0 : S // 2], late[:, S // 2 : S]])
        xb_bf = [
            late[:, S // 2 : S].bitcast(BF16),
            late[:, 3 * S // 4 : S].bitcast(BF16),
            sb("xb_bf2", [P, PACK * WIDTHS[2]], BF16)[:],
        ]
        xa_bf = sb("xa_bf", [P, PACK * M], BF16)
        xa_codes = [sb("xa_codes%d" % u, [P, M // 2], U32) for u in range(2)]
        xa_sc = [sb("xa_sc%d" % u, [P, M // 2], U8) for u in range(2)]
        xb_codes = [sb("xb_codes%d" % c, [P, w], U32) for c, w in enumerate(WIDTHS)]
        xb_sc = [sb("xb_sc%d" % c, [P, w], U8) for c, w in enumerate(WIDTHS)]

        def weave_a(u):
            dst, src = weave_views(xa_bf[:, u * 2 * M : (u + 1) * 2 * M], xa[:, :, u * M // 2 : (u + 1) * M // 2])
            nc.scalar.activation(out=dst, in_=src, func=ACT.Abs)

        def quantize_a(u):
            quantize(xa_codes[u][:], xa_sc[u][:], xa_bf[:, u * 2 * M : (u + 1) * 2 * M])

        def weave_b(c, engine_copy):
            dst, src = weave_views(xb_bf[c], xb[c].rearrange("p (t m) -> p t m", t=PACK))
            engine_copy(out=dst, in_=src)

        def quantize_b(c):
            quantize(xb_codes[c][:], xb_sc[c][:], xb_bf[c])

        def second_stage(c):
            width, start = WIDTHS[c], STARTS[c]
            tiles = N_TILES // len(OUT_BANKS[c])
            u, within = divmod(start, M // 2)
            a_cols = slice(within, within + width)
            operands = [
                (wa_codes, wa_sc, xa_codes[u][:, a_cols], xa_sc[u][:, a_cols]),
                (wb_codes, wb_sc, xb_codes[c][:], xb_sc[c][:]),
            ]
            for b, number in enumerate(OUT_BANKS[c]):
                acc = psum.tile([P, tiles, width], F32, name="acc_y", tag="bank%d" % number)
                for n, (codes, scales, x_codes, x_scales) in enumerate(operands):
                    for i in range(tiles):
                        cols = slice((tiles * b + i) * P, (tiles * b + i + 1) * P)
                        nc.tensor.matmul_mx(
                            out=acc[:, i, :], lhsT=codes[:, cols].bitcast(FP8X4), lhsT_scale=scales[:, cols],
                            rhs=x_codes.bitcast(FP8X4), rhs_scale=x_scales,
                            start=(n == 0 and i == 0), stop=(n == 1 and i == tiles - 1),
                        )
                y = sb("y%d_%d" % (c, b), [P, tiles, width], F32)
                vector_is_free = c == len(WIDTHS) - 1 and b == 1
                for i in range(tiles):
                    bias = bo_sb[:, tiles * b + i : tiles * b + i + 1]
                    if vector_is_free:
                        nc.vector.tensor_scalar(out=y[:, i, :], in0=acc[:, i, :], scalar1=bias, scalar2=None, op0=ALU.add)
                    else:
                        nc.scalar.activation(out=y[:, i, :], in_=acc[:, i, :], func=ACT.Identity, bias=bias)
                rows = out[tiles * b * P : tiles * (b + 1) * P, start : start + width]
                nc.sync.dma_start(out=rows.rearrange("(i p) m -> p i m", p=P), in_=y[:])

        weave_a(0)
        weave_b(0, nc.scalar.copy)
        weave_a(1)
        for t in range(PACK):
            pick_b(1, t)
        quantize_a(0)
        quantize_b(0)
        weave_b(1, nc.scalar.copy)
        second_stage(0)
        for t in range(PACK // 2):
            pick_b(2, t)
        quantize_a(1)
        quantize_b(1)
        second_stage(1)
        for t in range(PACK // 2, PACK):
            pick_b(2, t)
        weave_b(2, nc.vector.tensor_copy)
        quantize_b(2)
        second_stage(2)
